import numpy as np
import ml_dtypes


def mxq(x, axis, fmt="e4m3"):
    dtype, down = {"e4m3": (ml_dtypes.float8_e4m3fn, 7), "e5m2": (ml_dtypes.float8_e5m2, 14)}[fmt]
    v = np.moveaxis(np.asarray(x, np.float32).astype(ml_dtypes.bfloat16).astype(np.float64), axis, -1)
    blocks = v.reshape(v.shape[:-1] + (-1, 32))
    amax = np.abs(blocks).max(-1, keepdims=True)
    byte = np.maximum(np.where(amax > 0, np.frexp(amax)[1] - 1 + 127, 0) - down, 1)
    scale = np.exp2(byte - 127.0)
    codes = (blocks / scale).astype(np.float32).astype(dtype).astype(np.float64)
    return np.moveaxis((codes * scale).reshape(v.shape), -1, axis)


WIDE = False


def mx_kscale(k):
    if not WIDE:
        return np.ones(k)
    levels = np.array([10, -10, 5, -5, 0])
    if k % 512:
        return np.exp2(np.random.permutation(np.resize(levels, k // 32))).repeat(32)
    a = np.empty((k // 512, 16))
    for p in range(k // 512):
        a[p, :8] = np.random.permutation(np.resize(levels, 8))
        for g in range(8):
            far = levels[np.abs(levels - a[p, g]) >= 10]
            a[p, g + 8] = far[np.random.randint(len(far))]
    return np.exp2(a.ravel()).repeat(32)


def f64(x):
    return np.asarray(x).astype(np.float64)


def striped(idx):
    return np.tile(idx.reshape(-1, 16).T, (8, 1)).astype(np.uint16)


def unstriped(offs):
    return offs[:16].T.reshape(-1).astype(np.int64)


E2M1 = np.array([0.0, 0.5, 1.0, 1.5, 2.0, 3.0, 4.0, 6.0, -0.0, -0.5, -1.0, -1.5, -2.0, -3.0, -4.0, -6.0])


def pack_weight(w, fmt):
    k, n = w.shape
    w = f64(np.asarray(w, np.float32).astype(ml_dtypes.bfloat16)).reshape(k // 32, 32, n)
    amax = np.abs(w).max(1)
    if fmt == "e4m3":
        byte = np.frexp(amax)[1] - 1 + 127 - 7
    else:
        mant, ex = np.frexp(amax / 6.0)
        byte = np.where(mant > 0.5, ex, ex - 1) + 127
    byte = np.clip(np.where(amax > 0, byte, 1), 1, 254)
    scaled = (w * np.exp2(127.0 - byte)[:, None, :]).reshape(k, n).astype(np.float32)
    by_word = np.ascontiguousarray(scaled.reshape(k // 512, 128, 4, n).transpose(0, 1, 3, 2))
    if fmt == "e4m3":
        words = by_word.astype(ml_dtypes.float8_e4m3fn).view(np.uint8)
    else:
        c = by_word.astype(ml_dtypes.float4_e2m1fn).view(np.uint8) & 0xF
        words = (c[..., 0::2] | (c[..., 1::2] << 4)).reshape(k // 512, 128, 2 * n)
    return np.ascontiguousarray(words), np.ascontiguousarray(byte.astype(np.uint8).reshape(k // 512, 16, n))


def unpack_weight(words, scales, fmt):
    g, _, n = scales.shape
    words = np.ascontiguousarray(words).reshape(g, 128, n, -1)
    if fmt == "e4m3":
        vals = words.view(ml_dtypes.float8_e4m3fn).astype(np.float64)
    else:
        nib = np.empty((g, 128, n, 4), np.uint8)
        nib[..., 0::2] = words & 0xF
        nib[..., 1::2] = words >> 4
        vals = E2M1[nib]
    vals = vals * np.repeat(np.exp2(scales.astype(np.float64) - 127.0), 8, axis=1)[..., None]
    return vals.transpose(0, 1, 3, 2).reshape(g * 512, n)


def relu2(v):
    return np.maximum(v, 0.0) ** 2


K, T, E, C, N = 2560, 640, 6, 256, 256
R = 8


def by_expert(wq, xq):
    return np.concatenate([wq[e].T @ xq[:, e * C:(e + 1) * C] for e in range(E)], axis=1)


def setup_inputs():
    n = np.random.standard_normal
    s = mx_kscale(K)[:, None]
    slot_token = np.concatenate([r * (T // R) + np.random.permutation(T // R)[:C // R] for e in range(E) for r in range(R)])
    w = [pack_weight(m, "e2m1") for m in n((E, K, N)) / np.sqrt(K) / s[None]]
    return {
        "xT": (n((K, T)) * s).astype(np.float32),
        "w_words": np.stack([m[0] for m in w]),
        "w_scales": np.stack([m[1] for m in w]),
        "b": (0.3 * n((N, E))).astype(np.float32),
        "offs": striped(slot_token),
    }


def reference(xT, w_words, w_scales, b, offs):
    idx = unstriped(offs)
    w = np.stack([unpack_weight(w_words[e], w_scales[e], "e2m1") for e in range(E)])
    xq = mxq(f64(xT)[:, idx], 0, "e4m3")
    y = by_expert(w, xq)
    y = relu2(y + np.repeat(f64(b), C, axis=1))
    return y.reshape(N, E, R, C // R).transpose(0, 2, 1, 3).reshape(N, E * C)

@@ -1,0 +1,231 @@
+from contextlib import ExitStack
+
+import concourse.mybir as mybir
+
+K, T, E, C, N = 2560, 640, 6, 256, 256
+FLOPS = 2 * E * C * K * N
+
+F32 = mybir.dt.float32
+BF16 = mybir.dt.bfloat16
+I32 = mybir.dt.int32
+U32 = mybir.dt.uint32
+U16 = mybir.dt.uint16
+U8 = mybir.dt.uint8
+FP8X4 = mybir.dt.float8_e4m3fn_x4
+FP4X4 = mybir.dt.float4_e2m1fn_x4
+COPY = mybir.ActivationFunctionType.Copy
+RELU = mybir.ActivationFunctionType.Relu
+SQUARE = mybir.ActivationFunctionType.Square
+ADD = mybir.AluOpType.add
+MAX = mybir.AluOpType.max
+MULT = mybir.AluOpType.mult
+
+P = 128
+PASSES = K // 512
+SLOTS = E * C
+WINDOW = 704
+PAIR = 2 * C
+PACKS = ((0, 1, 2, 3), (4,))
+
+
+def tile_moe_eps_lin_relu2_kernel(tc, xT, w_words, w_scales, b, offs, out):
+    nc = tc.nc
+    with ExitStack() as ctx:
+        keep = ctx.enter_context(tc.tile_pool(name="keep", bufs=1))
+        psum = ctx.enter_context(tc.psum_pool(name="psum", bufs=8))
+
+        offsets = keep.tile([P, SLOTS // 16], U16, name="offsets")
+        nc.sync.dma_start(offsets[:], offs)
+
+        chunks = {0: ((0, 256), (256, 512), (512, 640)), 1: ((0, 384), (384, 640))}
+        raw = []
+        grouped = []
+        codes = []
+        words = []
+        for a in range(PASSES):
+            raw.append(keep.tile([P, 4, T], F32, name=f"raw{a}"))
+            grouped.append(keep.tile([P, T, 4], BF16, name=f"grouped{a}", align_bytes=64))
+            codes.append(keep.tile([P, WINDOW], I32, name=f"codes{a}", align_bytes=64))
+            words.append(keep.tile([P, SLOTS], U32, name=f"words{a}", align_bytes=64))
+        packed = []
+        gathered = []
+        for i in range(len(PACKS)):
+            packed.append(keep.tile([P, WINDOW], U8, name=f"packed{i}", align_bytes=64))
+            gathered.append(keep.tile([P, SLOTS], U8, name=f"gathered{i}", align_bytes=64))
+        planes = {}
+        for pack in PACKS:
+            for a in pack[1:]:
+                planes[a] = keep.tile([P, SLOTS], U8, name=f"plane{a}", align_bytes=64)
+
+        for a in range(PASSES):
+            rows = xT[512 * a : 512 * (a + 1), :].rearrange("(p j) t -> p j t", j=4)
+            for lo, hi in chunks.get(a, ((0, T),)):
+                nc.sync.dma_start(raw[a][:, :, lo:hi], rows[:, :, lo:hi])
+
+        w_plane = keep.tile([P, E * PASSES, N], U8, name="w_plane", align_bytes=64)
+        nc.gpsimd.memset(w_plane[:].rearrange("p g n -> p (g n)").bitcast(I32), 0)
+        for i in range(len(PACKS)):
+            nc.vector.memset(packed[i][:].bitcast(I32), 0)
+        for a in range(PASSES):
+            nc.vector.memset(codes[a][:, T:WINDOW], 0)
+        for a in planes:
+            nc.gpsimd.memset(planes[a][:].bitcast(I32), 0)
+
+        for q in range(4):
+            nc.sync.dma_start(
+                w_plane[32 * q : 32 * q + 4, :, :].rearrange("p g n -> p (g n)").bitcast(I32).rearrange("p (g n) -> p g n", n=N // 4),
+                w_scales[:, :, 4 * q : 4 * q + 4, :].rearrange("e a q n -> q (e a) n").bitcast(I32),
+            )
+        bias = keep.tile([P, 2, E], F32, name="bias")
+        nc.sync.dma_start(bias[:], b.rearrange("(h p) e -> p h e", p=P))
+        w_codes = []
+        for e in range(E):
+            w_codes.append(keep.tile([P, PASSES, 2 * N], U8, name=f"w_codes{e}", align_bytes=64))
+        for e in range(E):
+            nc.sync.dma_start(
+                w_codes[e][:].rearrange("p a n -> p (a n)").bitcast(I32).rearrange("p (a n) -> p a n", n=N // 2),
+                w_words[e].rearrange("a p n -> p a n").bitcast(I32),
+            )
+
+        def cast(a, lo, hi, on_vector):
+            dst = grouped[a][:, lo:hi, :]
+            src = raw[a][:, :, lo:hi].rearrange("p j t -> p t j")
+            if on_vector:
+                nc.vector.tensor_copy(out=dst, in_=src)
+            else:
+                nc.scalar.activation(dst, src, COPY)
+
+        def quantize(a, lo, hi):
+            i = 0 if a in PACKS[0] else 1
+            row = 4 * PACKS[i].index(a)
+            nc.vector.quantize_mx(
+                out=codes[a][:, lo:hi].bitcast(FP8X4),
+                scales=packed[i][row:P, lo:hi],
+                in_=grouped[a][:, lo:hi, :].rearrange("p t j -> p (t j)"),
+            )
+
+        def gather_words(a, lo, hi):
+            nc.vector.tensor_copy(words[a][:, lo:hi], codes[a][:].bitcast(U32).indirect(offsets[:, lo // 16 : hi // 16]))
+
+        def gather_bytes(i, lo, hi):
+            nc.vector.tensor_copy(gathered[i][:, lo:hi], packed[i][:].indirect(offsets[:, lo // 16 : hi // 16]))
+
+        def spread(lo, hi):
+            for j, a in enumerate(PACKS[0]):
+                if j:
+                    for q in range(4):
+                        nc.sync.dma_start(
+                            planes[a][32 * q : 32 * q + 4, lo:hi].bitcast(I32),
+                            gathered[0][32 * q + 4 * j : 32 * q + 4 * j + 4, lo:hi].bitcast(I32),
+                        )
+
+        def prepare(a):
+            quantize(a, 0, 512)
+            quantize(a, 512, T)
+
+        cast(0, 0, 256, True)
+        cast(0, 256, 512, True)
+        cast(0, 512, T, False)
+        quantize(0, 0, 256)
+        quantize(0, 256, 512)
+        quantize(0, 512, T)
+        cast(1, 0, 384, False)
+        cast(1, 384, T, False)
+        for a in range(2, PASSES):
+            cast(a, 0, T, False)
+        for p in range(3):
+            gather_words(0, PAIR * p, PAIR * (p + 1))
+        prepare(1)
+        for p in range(3):
+            gather_words(1, PAIR * p, PAIR * (p + 1))
+        def multiply(acc, e, h, half, a):
+            i = 0 if a in PACKS[0] else 1
+            scales = gathered[i] if a == PACKS[i][0] else planes[a]
+            cols = slice(C * e + 128 * half, C * e + 128 * (half + 1))
+            nc.tensor.matmul_mx(
+                out=acc,
+                lhsT=w_codes[e][:, a, N * h : N * (h + 1)].bitcast(FP4X4),
+                lhsT_scale=w_plane[:, PASSES * e + a, 128 * h : 128 * (h + 1)],
+                rhs=words[a][:, cols].bitcast(FP8X4),
+                rhs_scale=scales[:, cols],
+                start=(a == 0),
+                stop=(a == PASSES - 1),
+            )
+
+        out_view = out.rearrange("(h p) (m x) -> p h m x", p=P, m=8)
+        results = []
+        for p in range(3):
+            results.append(keep.tile([P, 2, 8, 2, 32], F32, name=f"result{p}"))
+
+        def square(e, h, relu):
+            nc.scalar.activation(results[e // 2][:, h, :, e % 2, :], relu[:].rearrange("p (m u) -> p m u", u=32), SQUARE)
+
+        def expert(e):
+            for h in range(2):
+                acc = psum.tile([P, 512], F32, name="acc")
+                for half in range(2):
+                    for a in range(PASSES):
+                        multiply(acc[:, 128 * half : 128 * (half + 1)], e, h, half, a)
+                relu = keep.tile([P, C], F32, name=f"relu{e}_{h}")
+                nc.scalar.activation(relu[:], acc[:, 0:C], RELU, bias=bias[:, h, e : e + 1])
+                square(e, h, relu)
+
+        def store(p):
+            for h in range(2):
+                nc.sync.dma_start(
+                    out_view[:, h, :, 64 * p : 64 * (p + 1)],
+                    results[p][:, h].rearrange("p m e u -> p m (e u)"),
+                )
+
+        prepare(2)
+        prepare(3)
+        gather_bytes(0, 0, PAIR)
+        spread(0, PAIR)
+        gather_words(2, 0, PAIR)
+        gather_words(3, 0, PAIR)
+        prepare(4)
+        gather_bytes(1, 0, PAIR)
+        gather_words(4, 0, C)
+        expert(0)
+        gather_words(4, C, 2 * C)
+        expert(1)
+        store(0)
+        gather_bytes(0, PAIR, 2 * PAIR)
+        gather_bytes(0, 2 * PAIR, 3 * PAIR)
+        spread(PAIR, SLOTS)
+        for e in (2, 3):
+            gather_words(2, C * e, C * (e + 1))
+            gather_words(3, C * e, C * (e + 1))
+            if e == 2:
+                gather_bytes(1, PAIR, 2 * PAIR)
+            gather_words(4, C * e, C * (e + 1))
+            expert(e)
+        store(1)
+        gather_bytes(1, 2 * PAIR, 3 * PAIR)
+        gather_words(2, 2 * PAIR, 3 * PAIR)
+        gather_words(3, 2 * PAIR, 3 * PAIR)
+        gather_words(4, 4 * C, 5 * C)
+        gather_words(4, 5 * C, 6 * C)
+        accs = {}
+        for a in range(PASSES):
+            for e in (4, 5):
+                for h in range(2):
+                    for half in range(2):
+                        if a == 0:
+                            accs[e, h, half] = psum.tile([P, 512], F32, name="acc")
+                        multiply(accs[e, h, half][:, 0:128], e, h, half, a)
+        for e in (4, 5):
+            for h in range(2):
+                relu = keep.tile([P, C], F32, name=f"relu{e}_{h}")
+                for half in range(2):
+                    part = relu[:, 128 * half : 128 * (half + 1)]
+                    if e == 5 and h == 1:
+                        nc.vector.tensor_scalar(part, accs[e, h, half][:, 0:128], bias[:, h, e : e + 1], 0.0, ADD, MAX)
+                    else:
+                        nc.scalar.activation(part, accs[e, h, half][:, 0:128], RELU, bias=bias[:, h, e : e + 1])
+                if e == 5 and h == 1:
+                    view = relu[:].rearrange("p (m u) -> p m u", u=32)
+                    nc.vector.tensor_tensor(results[2][:, h, :, 1, :], view, view, MULT)
+                else:
+                    square(e, h, relu)
+        store(2)

@@ -25,7 +25,8 @@ PASSES = K // 512
 SLOTS = E * C
 WINDOW = 704
 PAIR = 2 * C
-PACKS = ((0, 1, 2, 3), (4,))
+PACKS = ((0, 1, 2), (3, 4))
+PACK_OF = {a: i for i, pack in enumerate(PACKS) for a in pack}
 
 
 def tile_moe_eps_lin_relu2_kernel(tc, xT, w_words, w_scales, b, offs, out):
@@ -37,7 +38,7 @@ def tile_moe_eps_lin_relu2_kernel(tc, xT, w_words, w_scales, b, offs, out):
         offsets = keep.tile([P, SLOTS // 16], U16, name="offsets")
         nc.sync.dma_start(offsets[:], offs)
 
-        chunks = {0: ((0, 256), (256, 512), (512, 640)), 1: ((0, 384), (384, 640))}
+        chunks = {0: ((0, 384), (384, 640))}
         raw = []
         grouped = []
         codes = []
@@ -96,7 +97,7 @@ def tile_moe_eps_lin_relu2_kernel(tc, xT, w_words, w_scales, b, offs, out):
                 nc.scalar.activation(dst, src, COPY)
 
         def quantize(a, lo, hi):
-            i = 0 if a in PACKS[0] else 1
+            i = PACK_OF[a]
             row = 4 * PACKS[i].index(a)
             nc.vector.quantize_mx(
                 out=codes[a][:, lo:hi].bitcast(FP8X4),
@@ -110,28 +111,26 @@ def tile_moe_eps_lin_relu2_kernel(tc, xT, w_words, w_scales, b, offs, out):
         def gather_bytes(i, lo, hi):
             nc.vector.tensor_copy(gathered[i][:, lo:hi], packed[i][:].indirect(offsets[:, lo // 16 : hi // 16]))
 
-        def spread(lo, hi):
-            for j, a in enumerate(PACKS[0]):
+        def spread(i, lo, hi):
+            for j, a in enumerate(PACKS[i]):
                 if j:
                     for q in range(4):
                         nc.sync.dma_start(
                             planes[a][32 * q : 32 * q + 4, lo:hi].bitcast(I32),
-                            gathered[0][32 * q + 4 * j : 32 * q + 4 * j + 4, lo:hi].bitcast(I32),
+                            gathered[i][32 * q + 4 * j : 32 * q + 4 * j + 4, lo:hi].bitcast(I32),
                         )
 
         def prepare(a):
             quantize(a, 0, 512)
             quantize(a, 512, T)
 
-        cast(0, 0, 256, True)
-        cast(0, 256, 512, True)
-        cast(0, 512, T, False)
+        cast(0, 0, 384, True)
         quantize(0, 0, 256)
-        quantize(0, 256, 512)
-        quantize(0, 512, T)
-        cast(1, 0, 384, False)
-        cast(1, 384, T, False)
-        for a in range(2, PASSES):
+        quantize(0, 256, 384)
+        cast(0, 384, 512, True)
+        cast(0, 512, T, False)
+        quantize(0, 384, T)
+        for a in range(1, PASSES):
             cast(a, 0, T, False)
         for p in range(3):
             gather_words(0, PAIR * p, PAIR * (p + 1))
@@ -139,7 +138,7 @@ def tile_moe_eps_lin_relu2_kernel(tc, xT, w_words, w_scales, b, offs, out):
         for p in range(3):
             gather_words(1, PAIR * p, PAIR * (p + 1))
         def multiply(acc, e, h, half, a):
-            i = 0 if a in PACKS[0] else 1
+            i = PACK_OF[a]
             scales = gathered[i] if a == PACKS[i][0] else planes[a]
             cols = slice(C * e + 128 * half, C * e + 128 * (half + 1))
             nc.tensor.matmul_mx(
@@ -178,54 +177,64 @@ def tile_moe_eps_lin_relu2_kernel(tc, xT, w_words, w_scales, b, offs, out):
                 )
 
         prepare(2)
-        prepare(3)
-        gather_bytes(0, 0, PAIR)
-        spread(0, PAIR)
+        for p in range(3):
+            gather_bytes(0, PAIR * p, PAIR * (p + 1))
+        spread(0, 0, SLOTS)
         gather_words(2, 0, PAIR)
-        gather_words(3, 0, PAIR)
+        prepare(3)
         prepare(4)
         gather_bytes(1, 0, PAIR)
-        gather_words(4, 0, C)
-        expert(0)
-        gather_words(4, C, 2 * C)
-        expert(1)
-        store(0)
-        gather_bytes(0, PAIR, 2 * PAIR)
-        gather_bytes(0, 2 * PAIR, 3 * PAIR)
-        spread(PAIR, SLOTS)
-        for e in (2, 3):
-            gather_words(2, C * e, C * (e + 1))
-            gather_words(3, C * e, C * (e + 1))
-            if e == 2:
-                gather_bytes(1, PAIR, 2 * PAIR)
-            gather_words(4, C * e, C * (e + 1))
-            expert(e)
-        store(1)
-        gather_bytes(1, 2 * PAIR, 3 * PAIR)
-        gather_words(2, 2 * PAIR, 3 * PAIR)
-        gather_words(3, 2 * PAIR, 3 * PAIR)
-        gather_words(4, 4 * C, 5 * C)
-        gather_words(4, 5 * C, 6 * C)
-        accs = {}
-        for a in range(PASSES):
-            for e in (4, 5):
+        spread(1, 0, PAIR)
+        gather_words(3, 0, PAIR)
+
+        def open_pair(experts, upto):
+            for a in range(upto):
+                for e in experts:
+                    for h in range(2):
+                        for half in range(2):
+                            if a == 0:
+                                accs[e, h, half] = psum.tile([P, 512], F32, name="acc")
+                            multiply(accs[e, h, half][:, 0:128], e, h, half, a)
+
+        def close(e, first, last):
+            for a in range(first, PASSES):
                 for h in range(2):
                     for half in range(2):
-                        if a == 0:
-                            accs[e, h, half] = psum.tile([P, 512], F32, name="acc")
                         multiply(accs[e, h, half][:, 0:128], e, h, half, a)
-        for e in (4, 5):
             for h in range(2):
                 relu = keep.tile([P, C], F32, name=f"relu{e}_{h}")
                 for half in range(2):
                     part = relu[:, 128 * half : 128 * (half + 1)]
-                    if e == 5 and h == 1:
+                    if last and h == 1:
                         nc.vector.tensor_scalar(part, accs[e, h, half][:, 0:128], bias[:, h, e : e + 1], 0.0, ADD, MAX)
                     else:
                         nc.scalar.activation(part, accs[e, h, half][:, 0:128], RELU, bias=bias[:, h, e : e + 1])
-                if e == 5 and h == 1:
+                if last and h == 1:
                     view = relu[:].rearrange("p (m u) -> p m u", u=32)
                     nc.vector.tensor_tensor(results[2][:, h, :, 1, :], view, view, MULT)
                 else:
                     square(e, h, relu)
+
+        accs = {}
+        open_pair((0, 1), 3)
+        gather_words(4, 0, C)
+        close(0, 3, False)
+        gather_words(4, C, 2 * C)
+        close(1, 3, False)
+        store(0)
+        gather_bytes(1, PAIR, 2 * PAIR)
+        gather_bytes(1, 2 * PAIR, 3 * PAIR)
+        spread(1, PAIR, SLOTS)
+        for e in (2, 3):
+            for a in (2, 3, 4):
+                gather_words(a, C * e, C * (e + 1))
+            expert(e)
+        store(1)
+        gather_words(2, 2 * PAIR, 3 * PAIR)
+        gather_words(3, 2 * PAIR, 3 * PAIR)
+        open_pair((4, 5), 4)
+        gather_words(4, 4 * C, 5 * C)
+        close(4, 4, False)
+        gather_words(4, 5 * C, 6 * C)
+        close(5, 4, True)
         store(2)

@@ -25,6 +25,7 @@ PASSES = K // 512
 SLOTS = E * C
 WINDOW = 704
 PAIR = 2 * C
+LATE = (2, 3)
 PACKS = ((0, 1, 2), (3, 4))
 PACK_OF = {a: i for i, pack in enumerate(PACKS) for a in pack}
 
@@ -36,7 +37,6 @@ def tile_moe_eps_lin_relu2_kernel(tc, xT, w_words, w_scales, b, offs, out):
         psum = ctx.enter_context(tc.psum_pool(name="psum", bufs=8))
 
         offsets = keep.tile([P, SLOTS // 16], U16, name="offsets")
-        nc.sync.dma_start(offsets[:], offs)
 
         chunks = {0: ((0, 384), (384, 640))}
         raw = []
@@ -44,10 +44,10 @@ def tile_moe_eps_lin_relu2_kernel(tc, xT, w_words, w_scales, b, offs, out):
         codes = []
         words = []
         for a in range(PASSES):
-            raw.append(keep.tile([P, 4, T], F32, name=f"raw{a}"))
+            raw.append(keep.tile([P, 4, T], F32, name=f"raw{a}", tag=f"raw{a}", align_bytes=64))
             grouped.append(keep.tile([P, T, 4], BF16, name=f"grouped{a}", align_bytes=64))
             codes.append(keep.tile([P, WINDOW], I32, name=f"codes{a}", align_bytes=64))
-            words.append(keep.tile([P, SLOTS], U32, name=f"words{a}", align_bytes=64))
+            words.append(keep.tile([P, PAIR if a in LATE else SLOTS], U32, name=f"words{a}", align_bytes=64))
         packed = []
         gathered = []
         for i in range(len(PACKS)):
@@ -62,6 +62,8 @@ def tile_moe_eps_lin_relu2_kernel(tc, xT, w_words, w_scales, b, offs, out):
             rows = xT[512 * a : 512 * (a + 1), :].rearrange("(p j) t -> p j t", j=4)
             for lo, hi in chunks.get(a, ((0, T),)):
                 nc.sync.dma_start(raw[a][:, :, lo:hi], rows[:, :, lo:hi])
+            if a == 0:
+                nc.sync.dma_start(offsets[:], offs)
 
         w_plane = keep.tile([P, E * PASSES, N], U8, name="w_plane", align_bytes=64)
         nc.gpsimd.memset(w_plane[:].rearrange("p g n -> p (g n)").bitcast(I32), 0)
@@ -105,8 +107,13 @@ def tile_moe_eps_lin_relu2_kernel(tc, xT, w_words, w_scales, b, offs, out):
                 in_=grouped[a][:, lo:hi, :].rearrange("p t j -> p (t j)"),
             )
 
+        def slots(a, lo, hi):
+            if a in LATE and lo >= PAIR:
+                return late[:, LATE.index(a), lo - PAIR : hi - PAIR]
+            return words[a][:, lo:hi]
+
         def gather_words(a, lo, hi):
-            nc.vector.tensor_copy(words[a][:, lo:hi], codes[a][:].bitcast(U32).indirect(offsets[:, lo // 16 : hi // 16]))
+            nc.vector.tensor_copy(slots(a, lo, hi), codes[a][:].bitcast(U32).indirect(offsets[:, lo // 16 : hi // 16]))
 
         def gather_bytes(i, lo, hi):
             nc.vector.tensor_copy(gathered[i][:, lo:hi], packed[i][:].indirect(offsets[:, lo // 16 : hi // 16]))
@@ -130,8 +137,11 @@ def tile_moe_eps_lin_relu2_kernel(tc, xT, w_words, w_scales, b, offs, out):
         cast(0, 384, 512, True)
         cast(0, 512, T, False)
         quantize(0, 384, T)
-        for a in range(1, PASSES):
+        cast(1, 0, 512, False)
+        cast(1, 512, T, True)
+        for a in range(2, PASSES):
             cast(a, 0, T, False)
+        late = keep.tile([P, len(LATE), SLOTS - PAIR], U32, name="late", tag=f"raw{PASSES - 1}", align_bytes=64)
         for p in range(3):
             gather_words(0, PAIR * p, PAIR * (p + 1))
         prepare(1)
@@ -145,7 +155,7 @@ def tile_moe_eps_lin_relu2_kernel(tc, xT, w_words, w_scales, b, offs, out):
                 out=acc,
                 lhsT=w_codes[e][:, a, N * h : N * (h + 1)].bitcast(FP4X4),
                 lhsT_scale=w_plane[:, PASSES * e + a, 128 * h : 128 * (h + 1)],
-                rhs=words[a][:, cols].bitcast(FP8X4),
+                rhs=slots(a, cols.start, cols.stop).bitcast(FP8X4),
                 rhs_scale=scales[:, cols],
                 start=(a == 0),
                 stop=(a == PASSES - 1),
@@ -171,7 +181,8 @@ def tile_moe_eps_lin_relu2_kernel(tc, xT, w_words, w_scales, b, offs, out):
 
         def store(p):
             for h in range(2):
-                nc.sync.dma_start(
+                queue = nc.scalar if p == 2 and h == 0 else nc.sync
+                queue.dma_start(
                     out_view[:, h, :, 64 * p : 64 * (p + 1)],
                     results[p][:, h].rearrange("p m e u -> p m (e u)"),
                 )
@@ -231,10 +242,9 @@ def tile_moe_eps_lin_relu2_kernel(tc, xT, w_words, w_scales, b, offs, out):
             expert(e)
         store(1)
         gather_words(2, 2 * PAIR, 3 * PAIR)
-        gather_words(3, 2 * PAIR, 3 * PAIR)
-        open_pair((4, 5), 4)
-        gather_words(4, 4 * C, 5 * C)
-        close(4, 4, False)
-        gather_words(4, 5 * C, 6 * C)
-        close(5, 4, True)
+        open_pair((4, 5), 3)
+        for e in (4, 5):
+            for a in (3, 4):
+                gather_words(a, C * e, C * (e + 1))
+            close(e, 3, e == 5)
         store(2)

@@ -26,7 +26,7 @@ SLOTS = E * C
 WINDOW = 704
 PAIR = 2 * C
 LATE = (2, 3)
-PACKS = ((0, 1, 2), (3, 4))
+PACKS = ((0, 1, 2, 3), (4,))
 PACK_OF = {a: i for i, pack in enumerate(PACKS) for a in pack}
 
 
@@ -45,7 +45,7 @@ def tile_moe_eps_lin_relu2_kernel(tc, xT, w_words, w_scales, b, offs, out):
         words = []
         for a in range(PASSES):
             raw.append(keep.tile([P, 4, T], F32, name=f"raw{a}", tag=f"raw{a}", align_bytes=64))
-            grouped.append(keep.tile([P, T, 4], BF16, name=f"grouped{a}", align_bytes=64))
+            grouped.append(keep.tile([P, T, 4], BF16, name=f"grouped{a}", tag=f"grouped{a}", align_bytes=64))
             codes.append(keep.tile([P, WINDOW], I32, name=f"codes{a}", align_bytes=64))
             words.append(keep.tile([P, PAIR if a in LATE else SLOTS], U32, name=f"words{a}", align_bytes=64))
         packed = []
@@ -91,8 +91,8 @@ def tile_moe_eps_lin_relu2_kernel(tc, xT, w_words, w_scales, b, offs, out):
             )
 
         def cast(a, lo, hi, on_vector):
-            dst = grouped[a][:, lo:hi, :]
-            src = raw[a][:, :, lo:hi].rearrange("p j t -> p t j")
+            dst = grouped[a][:, lo:hi, :].rearrange("p (c i) j -> p c j i", i=4)
+            src = raw[a][:, :, lo:hi].rearrange("p j (c i) -> p c j i", i=4)
             if on_vector:
                 nc.vector.tensor_copy(out=dst, in_=src)
             else:
@@ -109,7 +109,7 @@ def tile_moe_eps_lin_relu2_kernel(tc, xT, w_words, w_scales, b, offs, out):
 
         def slots(a, lo, hi):
             if a in LATE and lo >= PAIR:
-                return late[:, LATE.index(a), lo - PAIR : hi - PAIR]
+                return late[:, a - 2, lo - PAIR : hi - PAIR]
             return words[a][:, lo:hi]
 
         def gather_words(a, lo, hi):
@@ -118,14 +118,9 @@ def tile_moe_eps_lin_relu2_kernel(tc, xT, w_words, w_scales, b, offs, out):
         def gather_bytes(i, lo, hi):
             nc.vector.tensor_copy(gathered[i][:, lo:hi], packed[i][:].indirect(offsets[:, lo // 16 : hi // 16]))
 
-        def spread(i, lo, hi):
-            for j, a in enumerate(PACKS[i]):
-                if j:
-                    for q in range(4):
-                        nc.sync.dma_start(
-                            planes[a][32 * q : 32 * q + 4, lo:hi].bitcast(I32),
-                            gathered[i][32 * q + 4 * j : 32 * q + 4 * j + 4, lo:hi].bitcast(I32),
-                        )
+        def spread(lo, hi):
+            for j in (1, 2, 3):
+                nc.sync.dma_start(planes[j][0:100, lo:hi].bitcast(I32), gathered[0][4 * j : 100 + 4 * j, lo:hi].bitcast(I32))
 
         def prepare(a):
             quantize(a, 0, 512)
@@ -141,7 +136,7 @@ def tile_moe_eps_lin_relu2_kernel(tc, xT, w_words, w_scales, b, offs, out):
         cast(1, 512, T, True)
         for a in range(2, PASSES):
             cast(a, 0, T, False)
-        late = keep.tile([P, len(LATE), SLOTS - PAIR], U32, name="late", tag=f"raw{PASSES - 1}", align_bytes=64)
+        late = keep.tile([P, 2, SLOTS - PAIR], U32, name="late", tag=f"raw{PASSES - 1}", align_bytes=64)
         for p in range(3):
             gather_words(0, PAIR * p, PAIR * (p + 1))
         prepare(1)
@@ -149,14 +144,14 @@ def tile_moe_eps_lin_relu2_kernel(tc, xT, w_words, w_scales, b, offs, out):
             gather_words(1, PAIR * p, PAIR * (p + 1))
         def multiply(acc, e, h, half, a):
             i = PACK_OF[a]
-            scales = gathered[i] if a == PACKS[i][0] else planes[a]
             cols = slice(C * e + 128 * half, C * e + 128 * (half + 1))
+            scales = gathered[i][:, cols] if a == PACKS[i][0] else planes[a][:, cols]
             nc.tensor.matmul_mx(
                 out=acc,
                 lhsT=w_codes[e][:, a, N * h : N * (h + 1)].bitcast(FP4X4),
                 lhsT_scale=w_plane[:, PASSES * e + a, 128 * h : 128 * (h + 1)],
                 rhs=slots(a, cols.start, cols.stop).bitcast(FP8X4),
-                rhs_scale=scales[:, cols],
+                rhs_scale=scales,
                 start=(a == 0),
                 stop=(a == PASSES - 1),
             )
@@ -169,34 +164,22 @@ def tile_moe_eps_lin_relu2_kernel(tc, xT, w_words, w_scales, b, offs, out):
         def square(e, h, relu):
             nc.scalar.activation(results[e // 2][:, h, :, e % 2, :], relu[:].rearrange("p (m u) -> p m u", u=32), SQUARE)
 
-        def expert(e):
-            for h in range(2):
-                acc = psum.tile([P, 512], F32, name="acc")
-                for half in range(2):
-                    for a in range(PASSES):
-                        multiply(acc[:, 128 * half : 128 * (half + 1)], e, h, half, a)
-                relu = keep.tile([P, C], F32, name=f"relu{e}_{h}")
-                nc.scalar.activation(relu[:], acc[:, 0:C], RELU, bias=bias[:, h, e : e + 1])
-                square(e, h, relu)
-
         def store(p):
             for h in range(2):
-                queue = nc.scalar if p == 2 and h == 0 else nc.sync
-                queue.dma_start(
+                nc.sync.dma_start(
                     out_view[:, h, :, 64 * p : 64 * (p + 1)],
                     results[p][:, h].rearrange("p m e u -> p m (e u)"),
                 )
 
         prepare(2)
-        for p in range(3):
-            gather_bytes(0, PAIR * p, PAIR * (p + 1))
-        spread(0, 0, SLOTS)
         gather_words(2, 0, PAIR)
         prepare(3)
+        gather_bytes(0, 0, PAIR)
+        spread(0, PAIR)
+        gather_bytes(0, PAIR, 2 * PAIR)
+        gather_bytes(0, 2 * PAIR, 3 * PAIR)
+        spread(PAIR, SLOTS)
         prepare(4)
-        gather_bytes(1, 0, PAIR)
-        spread(1, 0, PAIR)
-        gather_words(3, 0, PAIR)
 
         def open_pair(experts, upto):
             for a in range(upto):
@@ -227,24 +210,22 @@ def tile_moe_eps_lin_relu2_kernel(tc, xT, w_words, w_scales, b, offs, out):
                     square(e, h, relu)
 
         accs = {}
-        open_pair((0, 1), 3)
-        gather_words(4, 0, C)
-        close(0, 3, False)
-        gather_words(4, C, 2 * C)
-        close(1, 3, False)
-        store(0)
-        gather_bytes(1, PAIR, 2 * PAIR)
-        gather_bytes(1, 2 * PAIR, 3 * PAIR)
-        spread(1, PAIR, SLOTS)
-        for e in (2, 3):
-            for a in (2, 3, 4):
-                gather_words(a, C * e, C * (e + 1))
-            expert(e)
-        store(1)
-        gather_words(2, 2 * PAIR, 3 * PAIR)
-        open_pair((4, 5), 3)
-        for e in (4, 5):
-            for a in (3, 4):
-                gather_words(a, C * e, C * (e + 1))
-            close(e, 3, e == 5)
-        store(2)
+        for p in range(3):
+            pair = (2 * p, 2 * p + 1)
+            gather_bytes(1, PAIR * p, PAIR * (p + 1))
+            if p:
+                gather_words(2, PAIR * p, PAIR * (p + 1))
+            gather_words(3, PAIR * p, PAIR * (p + 1))
+            open_pair(pair, 4)
+            for e in pair:
+                gather_words(4, C * e, C * (e + 1))
+                close(e, 4, e == 5)
+                if p == 2:
+                    for h in range(2):
+                        queue = nc.scalar if e == 5 and h == 0 else nc.sync
+                        queue.dma_start(
+                            out_view[:, h, :, 32 * e : 32 * (e + 1)],
+                            results[2][:, h, :, e - 4, :],
+                        )
+            if p < 2:
+                store(p)

@@ -23,9 +23,11 @@ MULT = mybir.AluOpType.mult
 P = 128
 PASSES = K // 512
 SLOTS = E * C
-WINDOW = 704
+WINDOWS = (1408, 1408, 1408, 704, 704)
+BYTE_WINDOWS = (1408, 704)
 PAIR = 2 * C
-LATE = (2, 3)
+LATE = {2: 2 * PAIR, 3: PAIR}
+W_LOADS = ((0, 2), (2, 6))
 PACKS = ((0, 1, 2, 3), (4,))
 PACK_OF = {a: i for i, pack in enumerate(PACKS) for a in pack}
 
@@ -46,12 +48,12 @@ def tile_moe_eps_lin_relu2_kernel(tc, xT, w_words, w_scales, b, offs, out):
         for a in range(PASSES):
             raw.append(keep.tile([P, 4, T], F32, name=f"raw{a}", tag=f"raw{a}", align_bytes=64))
             grouped.append(keep.tile([P, T, 4], BF16, name=f"grouped{a}", tag=f"grouped{a}", align_bytes=64))
-            codes.append(keep.tile([P, WINDOW], I32, name=f"codes{a}", align_bytes=64))
-            words.append(keep.tile([P, PAIR if a in LATE else SLOTS], U32, name=f"words{a}", align_bytes=64))
+            codes.append(keep.tile([P, WINDOWS[a]], I32, name=f"codes{a}", align_bytes=64))
+            words.append(keep.tile([P, LATE.get(a, SLOTS)], U32, name=f"words{a}", align_bytes=64))
         packed = []
         gathered = []
         for i in range(len(PACKS)):
-            packed.append(keep.tile([P, WINDOW], U8, name=f"packed{i}", align_bytes=64))
+            packed.append(keep.tile([P, BYTE_WINDOWS[i]], U8, name=f"packed{i}", align_bytes=64))
             gathered.append(keep.tile([P, SLOTS], U8, name=f"gathered{i}", align_bytes=64))
         planes = {}
         for pack in PACKS:
@@ -70,7 +72,8 @@ def tile_moe_eps_lin_relu2_kernel(tc, xT, w_words, w_scales, b, offs, out):
         for i in range(len(PACKS)):
             nc.vector.memset(packed[i][:].bitcast(I32), 0)
         for a in range(PASSES):
-            nc.vector.memset(codes[a][:, T:WINDOW], 0)
+            engine = nc.gpsimd if a == 2 else nc.vector
+            engine.memset(codes[a][:, T : WINDOWS[a]], 0)
         for a in planes:
             nc.gpsimd.memset(planes[a][:].bitcast(I32), 0)
 
@@ -82,17 +85,17 @@ def tile_moe_eps_lin_relu2_kernel(tc, xT, w_words, w_scales, b, offs, out):
         bias = keep.tile([P, 2, E], F32, name="bias")
         nc.sync.dma_start(bias[:], b.rearrange("(h p) e -> p h e", p=P))
         w_codes = []
-        for e in range(E):
-            w_codes.append(keep.tile([P, PASSES, 2 * N], U8, name=f"w_codes{e}", align_bytes=64))
-        for e in range(E):
+        for first, last in W_LOADS:
+            w_codes.append(keep.tile([P, (last - first) * PASSES, 2 * N], U8, name=f"w_codes{first}", align_bytes=64))
+        for i, (first, last) in enumerate(W_LOADS):
             nc.sync.dma_start(
-                w_codes[e][:].rearrange("p a n -> p (a n)").bitcast(I32).rearrange("p (a n) -> p a n", n=N // 2),
-                w_words[e].rearrange("a p n -> p a n").bitcast(I32),
+                w_codes[i][:].rearrange("p g n -> p (g n)").bitcast(I32).rearrange("p (g n) -> p g n", n=N // 2),
+                w_words[first:last].rearrange("e a p n -> p (e a) n").bitcast(I32),
             )
 
         def cast(a, lo, hi, on_vector):
-            dst = grouped[a][:, lo:hi, :].rearrange("p (c i) j -> p c j i", i=4)
-            src = raw[a][:, :, lo:hi].rearrange("p j (c i) -> p c j i", i=4)
+            dst = grouped[a][:, lo:hi, :]
+            src = raw[a][:, :, lo:hi].rearrange("p j t -> p t j")
             if on_vector:
                 nc.vector.tensor_copy(out=dst, in_=src)
             else:
@@ -108,7 +111,7 @@ def tile_moe_eps_lin_relu2_kernel(tc, xT, w_words, w_scales, b, offs, out):
             )
 
         def slots(a, lo, hi):
-            if a in LATE and lo >= PAIR:
+            if lo >= LATE.get(a, SLOTS):
                 return late[:, a - 2, lo - PAIR : hi - PAIR]
             return words[a][:, lo:hi]
 
@@ -132,23 +135,24 @@ def tile_moe_eps_lin_relu2_kernel(tc, xT, w_words, w_scales, b, offs, out):
         cast(0, 384, 512, True)
         cast(0, 512, T, False)
         quantize(0, 384, T)
-        cast(1, 0, 512, False)
-        cast(1, 512, T, True)
+        cast(1, 0, 384, False)
+        cast(1, 384, T, True)
         for a in range(2, PASSES):
             cast(a, 0, T, False)
         late = keep.tile([P, 2, SLOTS - PAIR], U32, name="late", tag=f"raw{PASSES - 1}", align_bytes=64)
-        for p in range(3):
-            gather_words(0, PAIR * p, PAIR * (p + 1))
+        gather_words(0, 0, 2 * PAIR)
+        gather_words(0, 2 * PAIR, SLOTS)
         prepare(1)
-        for p in range(3):
-            gather_words(1, PAIR * p, PAIR * (p + 1))
+        gather_words(1, 0, 2 * PAIR)
+        gather_words(1, 2 * PAIR, SLOTS)
         def multiply(acc, e, h, half, a):
             i = PACK_OF[a]
+            w = 0 if e < W_LOADS[0][1] else 1
             cols = slice(C * e + 128 * half, C * e + 128 * (half + 1))
             scales = gathered[i][:, cols] if a == PACKS[i][0] else planes[a][:, cols]
             nc.tensor.matmul_mx(
                 out=acc,
-                lhsT=w_codes[e][:, a, N * h : N * (h + 1)].bitcast(FP4X4),
+                lhsT=w_codes[w][:, PASSES * (e - W_LOADS[w][0]) + a, N * h : N * (h + 1)].bitcast(FP4X4),
                 lhsT_scale=w_plane[:, PASSES * e + a, 128 * h : 128 * (h + 1)],
                 rhs=slots(a, cols.start, cols.stop).bitcast(FP8X4),
                 rhs_scale=scales,
@@ -164,20 +168,18 @@ def tile_moe_eps_lin_relu2_kernel(tc, xT, w_words, w_scales, b, offs, out):
         def square(e, h, relu):
             nc.scalar.activation(results[e // 2][:, h, :, e % 2, :], relu[:].rearrange("p (m u) -> p m u", u=32), SQUARE)
 
-        def store(p):
-            for h in range(2):
-                nc.sync.dma_start(
-                    out_view[:, h, :, 64 * p : 64 * (p + 1)],
-                    results[p][:, h].rearrange("p m e u -> p m (e u)"),
-                )
+        def store(p, h, m0, m1, queue):
+            queue.dma_start(
+                out_view[:, h, m0:m1, 64 * p : 64 * (p + 1)],
+                results[p][:, h, m0:m1].rearrange("p m e u -> p m (e u)"),
+            )
 
         prepare(2)
-        gather_words(2, 0, PAIR)
+        gather_words(2, 0, 2 * PAIR)
         prepare(3)
         gather_bytes(0, 0, PAIR)
         spread(0, PAIR)
-        gather_bytes(0, PAIR, 2 * PAIR)
-        gather_bytes(0, 2 * PAIR, 3 * PAIR)
+        gather_bytes(0, PAIR, SLOTS)
         spread(PAIR, SLOTS)
         prepare(4)
 
@@ -190,42 +192,48 @@ def tile_moe_eps_lin_relu2_kernel(tc, xT, w_words, w_scales, b, offs, out):
                                 accs[e, h, half] = psum.tile([P, 512], F32, name="acc")
                             multiply(accs[e, h, half][:, 0:128], e, h, half, a)
 
-        def close(e, first, last):
-            for a in range(first, PASSES):
-                for h in range(2):
-                    for half in range(2):
-                        multiply(accs[e, h, half][:, 0:128], e, h, half, a)
+        def close(e):
+            gather_words(4, C * e, C * (e + 1))
+            for h in range(2):
+                for half in range(2):
+                    multiply(accs[e, h, half][:, 0:128], e, h, half, PASSES - 1)
             for h in range(2):
                 relu = keep.tile([P, C], F32, name=f"relu{e}_{h}")
                 for half in range(2):
                     part = relu[:, 128 * half : 128 * (half + 1)]
-                    if last and h == 1:
-                        nc.vector.tensor_scalar(part, accs[e, h, half][:, 0:128], bias[:, h, e : e + 1], 0.0, ADD, MAX)
-                    else:
-                        nc.scalar.activation(part, accs[e, h, half][:, 0:128], RELU, bias=bias[:, h, e : e + 1])
-                if last and h == 1:
+                    nc.scalar.activation(part, accs[e, h, half][:, 0:128], RELU, bias=bias[:, h, e : e + 1])
+                square(e, h, relu)
+
+        def close_last(e):
+            for half in range(2):
+                gather_words(4, C * e + 128 * half, C * e + 128 * (half + 1))
+            for half in range(2):
+                for h in range(2):
+                    multiply(accs[e, h, half][:, 0:128], e, h, half, PASSES - 1)
+                for h in range(2):
+                    relu = keep.tile([P, 128], F32, name=f"relu{e}_{h}_{half}")
                     view = relu[:].rearrange("p (m u) -> p m u", u=32)
-                    nc.vector.tensor_tensor(results[2][:, h, :, 1, :], view, view, MULT)
-                else:
-                    square(e, h, relu)
+                    dst = results[e // 2][:, h, 4 * half : 4 * (half + 1), e % 2, :]
+                    if h == 0:
+                        nc.scalar.activation(relu[:], accs[e, h, half][:, 0:128], RELU, bias=bias[:, h, e : e + 1])
+                        nc.scalar.activation(dst, view, SQUARE)
+                    else:
+                        nc.vector.tensor_scalar(relu[:], accs[e, h, half][:, 0:128], bias[:, h, e : e + 1], 0.0, ADD, MAX)
+                        nc.vector.tensor_tensor(dst, view, view, MULT)
+                for h in range(2):
+                    store(e // 2, h, 4 * half, 4 * (half + 1), nc.scalar if h == 0 and half == 1 else nc.sync)
 
         accs = {}
         for p in range(3):
-            pair = (2 * p, 2 * p + 1)
-            gather_bytes(1, PAIR * p, PAIR * (p + 1))
-            if p:
+            if p == 2:
                 gather_words(2, PAIR * p, PAIR * (p + 1))
             gather_words(3, PAIR * p, PAIR * (p + 1))
-            open_pair(pair, 4)
-            for e in pair:
-                gather_words(4, C * e, C * (e + 1))
-                close(e, 4, e == 5)
-                if p == 2:
-                    for h in range(2):
-                        queue = nc.scalar if e == 5 and h == 0 else nc.sync
-                        queue.dma_start(
-                            out_view[:, h, :, 32 * e : 32 * (e + 1)],
-                            results[2][:, h, :, e - 4, :],
-                        )
+            gather_bytes(1, PAIR * p, PAIR * (p + 1))
+            open_pair((2 * p, 2 * p + 1), 4)
+            close(2 * p)
             if p < 2:
-                store(p)
+                close(2 * p + 1)
+                for h in range(2):
+                    store(p, h, 0, 8, nc.sync)
+            else:
+                close_last(2 * p + 1)

from contextlib import ExitStack

import concourse.mybir as mybir

K, T, E, C, N = 2560, 640, 6, 256, 256
FLOPS = 2 * E * C * K * N

F32 = mybir.dt.float32
BF16 = mybir.dt.bfloat16
I32 = mybir.dt.int32
U32 = mybir.dt.uint32
U16 = mybir.dt.uint16
U8 = mybir.dt.uint8
FP8X4 = mybir.dt.float8_e4m3fn_x4
FP4X4 = mybir.dt.float4_e2m1fn_x4
COPY = mybir.ActivationFunctionType.Copy
RELU = mybir.ActivationFunctionType.Relu
SQUARE = mybir.ActivationFunctionType.Square
ADD = mybir.AluOpType.add
MAX = mybir.AluOpType.max
MULT = mybir.AluOpType.mult

P = 128
PASSES = K // 512
SLOTS = E * C
WINDOWS = (1408, 1408, 1408, 704, 704)
BYTE_WINDOWS = (1408, 704)
PAIR = 2 * C
LATE = {2: 2 * PAIR, 3: PAIR}
W_LOADS = ((0, 2), (2, 6))
PACKS = ((0, 1, 2, 3), (4,))
PACK_OF = {a: i for i, pack in enumerate(PACKS) for a in pack}


def tile_moe_eps_lin_relu2_kernel(tc, xT, w_words, w_scales, b, offs, out):
    nc = tc.nc
    with ExitStack() as ctx:
        keep = ctx.enter_context(tc.tile_pool(name="keep", bufs=1))
        psum = ctx.enter_context(tc.psum_pool(name="psum", bufs=8))

        offsets = keep.tile([P, SLOTS // 16], U16, name="offsets")

        chunks = {0: ((0, 384), (384, 640))}
        raw = []
        grouped = []
        codes = []
        words = []
        for a in range(PASSES):
            raw.append(keep.tile([P, 4, T], F32, name=f"raw{a}", tag=f"raw{a}", align_bytes=64))
            grouped.append(keep.tile([P, T, 4], BF16, name=f"grouped{a}", tag=f"grouped{a}", align_bytes=64))
            codes.append(keep.tile([P, WINDOWS[a]], I32, name=f"codes{a}", align_bytes=64))
            words.append(keep.tile([P, LATE.get(a, SLOTS)], U32, name=f"words{a}", align_bytes=64))
        packed = []
        gathered = []
        for i in range(len(PACKS)):
            packed.append(keep.tile([P, BYTE_WINDOWS[i]], U8, name=f"packed{i}", align_bytes=64))
            gathered.append(keep.tile([P, SLOTS], U8, name=f"gathered{i}", align_bytes=64))
        planes = {}
        for pack in PACKS:
            for a in pack[1:]:
                planes[a] = keep.tile([P, SLOTS], U8, name=f"plane{a}", align_bytes=64)

        for a in range(PASSES):
            rows = xT[512 * a : 512 * (a + 1), :].rearrange("(p j) t -> p j t", j=4)
            for lo, hi in chunks.get(a, ((0, T),)):
                nc.sync.dma_start(raw[a][:, :, lo:hi], rows[:, :, lo:hi])
            if a == 0:
                nc.sync.dma_start(offsets[:], offs)

        w_plane = keep.tile([P, E * PASSES, N], U8, name="w_plane", align_bytes=64)
        nc.gpsimd.memset(w_plane[:].rearrange("p g n -> p (g n)").bitcast(I32), 0)
        for i in range(len(PACKS)):
            nc.vector.memset(packed[i][:].bitcast(I32), 0)
        for a in range(PASSES):
            engine = nc.gpsimd if a == 2 else nc.vector
            engine.memset(codes[a][:, T : WINDOWS[a]], 0)
        for a in planes:
            nc.gpsimd.memset(planes[a][:].bitcast(I32), 0)

        for q in range(4):
            nc.sync.dma_start(
                w_plane[32 * q : 32 * q + 4, :, :].rearrange("p g n -> p (g n)").bitcast(I32).rearrange("p (g n) -> p g n", n=N // 4),
                w_scales[:, :, 4 * q : 4 * q + 4, :].rearrange("e a q n -> q (e a) n").bitcast(I32),
            )
        bias = keep.tile([P, 2, E], F32, name="bias")
        nc.sync.dma_start(bias[:], b.rearrange("(h p) e -> p h e", p=P))
        w_codes = []
        for first, last in W_LOADS:
            w_codes.append(keep.tile([P, (last - first) * PASSES, 2 * N], U8, name=f"w_codes{first}", align_bytes=64))
        for i, (first, last) in enumerate(W_LOADS):
            nc.sync.dma_start(
                w_codes[i][:].rearrange("p g n -> p (g n)").bitcast(I32).rearrange("p (g n) -> p g n", n=N // 2),
                w_words[first:last].rearrange("e a p n -> p (e a) n").bitcast(I32),
            )

        def cast(a, lo, hi, on_vector):
            dst = grouped[a][:, lo:hi, :]
            src = raw[a][:, :, lo:hi].rearrange("p j t -> p t j")
            if on_vector:
                nc.vector.tensor_copy(out=dst, in_=src)
            else:
                nc.scalar.activation(dst, src, COPY)

        def quantize(a, lo, hi):
            i = PACK_OF[a]
            row = 4 * PACKS[i].index(a)
            nc.vector.quantize_mx(
                out=codes[a][:, lo:hi].bitcast(FP8X4),
                scales=packed[i][row:P, lo:hi],
                in_=grouped[a][:, lo:hi, :].rearrange("p t j -> p (t j)"),
            )

        def slots(a, lo, hi):
            if lo >= LATE.get(a, SLOTS):
                return late[:, a - 2, lo - PAIR : hi - PAIR]
            return words[a][:, lo:hi]

        def gather_words(a, lo, hi):
            nc.vector.tensor_copy(slots(a, lo, hi), codes[a][:].bitcast(U32).indirect(offsets[:, lo // 16 : hi // 16]))

        def gather_bytes(i, lo, hi):
            nc.vector.tensor_copy(gathered[i][:, lo:hi], packed[i][:].indirect(offsets[:, lo // 16 : hi // 16]))

        def spread(lo, hi):
            for j in (1, 2, 3):
                nc.sync.dma_start(planes[j][0:100, lo:hi].bitcast(I32), gathered[0][4 * j : 100 + 4 * j, lo:hi].bitcast(I32))

        def prepare(a):
            quantize(a, 0, 512)
            quantize(a, 512, T)

        cast(0, 0, 384, True)
        quantize(0, 0, 256)
        quantize(0, 256, 384)
        cast(0, 384, 512, True)
        cast(0, 512, T, False)
        quantize(0, 384, T)
        cast(1, 0, 384, False)
        cast(1, 384, T, True)
        for a in range(2, PASSES):
            cast(a, 0, T, False)
        late = keep.tile([P, 2, SLOTS - PAIR], U32, name="late", tag=f"raw{PASSES - 1}", align_bytes=64)
        gather_words(0, 0, 2 * PAIR)
        gather_words(0, 2 * PAIR, SLOTS)
        prepare(1)
        gather_words(1, 0, 2 * PAIR)
        gather_words(1, 2 * PAIR, SLOTS)
        def multiply(acc, e, h, half, a):
            i = PACK_OF[a]
            w = 0 if e < W_LOADS[0][1] else 1
            cols = slice(C * e + 128 * half, C * e + 128 * (half + 1))
            scales = gathered[i][:, cols] if a == PACKS[i][0] else planes[a][:, cols]
            nc.tensor.matmul_mx(
                out=acc,
                lhsT=w_codes[w][:, PASSES * (e - W_LOADS[w][0]) + a, N * h : N * (h + 1)].bitcast(FP4X4),
                lhsT_scale=w_plane[:, PASSES * e + a, 128 * h : 128 * (h + 1)],
                rhs=slots(a, cols.start, cols.stop).bitcast(FP8X4),
                rhs_scale=scales,
                start=(a == 0),
                stop=(a == PASSES - 1),
            )

        out_view = out.rearrange("(h p) (m x) -> p h m x", p=P, m=8)
        results = []
        for p in range(3):
            results.append(keep.tile([P, 2, 8, 2, 32], F32, name=f"result{p}"))

        def square(e, h, relu):
            nc.scalar.activation(results[e // 2][:, h, :, e % 2, :], relu[:].rearrange("p (m u) -> p m u", u=32), SQUARE)

        def store(p, h, m0, m1, queue):
            queue.dma_start(
                out_view[:, h, m0:m1, 64 * p : 64 * (p + 1)],
                results[p][:, h, m0:m1].rearrange("p m e u -> p m (e u)"),
            )

        prepare(2)
        gather_words(2, 0, 2 * PAIR)
        prepare(3)
        gather_bytes(0, 0, PAIR)
        spread(0, PAIR)
        gather_bytes(0, PAIR, SLOTS)
        spread(PAIR, SLOTS)
        prepare(4)

        def open_pair(experts, upto):
            for a in range(upto):
                for e in experts:
                    for h in range(2):
                        for half in range(2):
                            if a == 0:
                                accs[e, h, half] = psum.tile([P, 512], F32, name="acc")
                            multiply(accs[e, h, half][:, 0:128], e, h, half, a)

        def close(e):
            gather_words(4, C * e, C * (e + 1))
            for h in range(2):
                for half in range(2):
                    multiply(accs[e, h, half][:, 0:128], e, h, half, PASSES - 1)
            for h in range(2):
                relu = keep.tile([P, C], F32, name=f"relu{e}_{h}")
                for half in range(2):
                    part = relu[:, 128 * half : 128 * (half + 1)]
                    nc.scalar.activation(part, accs[e, h, half][:, 0:128], RELU, bias=bias[:, h, e : e + 1])
                square(e, h, relu)

        def close_last(e):
            for half in range(2):
                gather_words(4, C * e + 128 * half, C * e + 128 * (half + 1))
            for half in range(2):
                for h in range(2):
                    multiply(accs[e, h, half][:, 0:128], e, h, half, PASSES - 1)
                for h in range(2):
                    relu = keep.tile([P, 128], F32, name=f"relu{e}_{h}_{half}")
                    view = relu[:].rearrange("p (m u) -> p m u", u=32)
                    dst = results[e // 2][:, h, 4 * half : 4 * (half + 1), e % 2, :]
                    if h == 0:
                        nc.scalar.activation(relu[:], accs[e, h, half][:, 0:128], RELU, bias=bias[:, h, e : e + 1])
                        nc.scalar.activation(dst, view, SQUARE)
                    else:
                        nc.vector.tensor_scalar(relu[:], accs[e, h, half][:, 0:128], bias[:, h, e : e + 1], 0.0, ADD, MAX)
                        nc.vector.tensor_tensor(dst, view, view, MULT)
                for h in range(2):
                    store(e // 2, h, 4 * half, 4 * (half + 1), nc.scalar if h == 0 and half == 1 else nc.sync)

        accs = {}
        for p in range(3):
            if p == 2:
                gather_words(2, PAIR * p, PAIR * (p + 1))
            gather_words(3, PAIR * p, PAIR * (p + 1))
            gather_bytes(1, PAIR * p, PAIR * (p + 1))
            open_pair((2 * p, 2 * p + 1), 4)
            close(2 * p)
            if p < 2:
                close(2 * p + 1)
                for h in range(2):
                    store(p, h, 0, 8, nc.sync)
            else:
                close_last(2 * p + 1)
